import numpy as np
import ml_dtypes


def mxq(x, axis, fmt="e4m3"):
    dtype, down = {"e4m3": (ml_dtypes.float8_e4m3fn, 7), "e5m2": (ml_dtypes.float8_e5m2, 14)}[fmt]
    v = np.moveaxis(np.asarray(x, np.float32).astype(ml_dtypes.bfloat16).astype(np.float64), axis, -1)
    blocks = v.reshape(v.shape[:-1] + (-1, 32))
    amax = np.abs(blocks).max(-1, keepdims=True)
    byte = np.maximum(np.where(amax > 0, np.frexp(amax)[1] - 1 + 127, 0) - down, 1)
    scale = np.exp2(byte - 127.0)
    codes = (blocks / scale).astype(np.float32).astype(dtype).astype(np.float64)
    return np.moveaxis((codes * scale).reshape(v.shape), -1, axis)


WIDE = False


def mx_kscale(k):
    if not WIDE:
        return np.ones(k)
    levels = np.array([30, -30])
    if k % 512:
        return np.exp2(np.random.permutation(np.resize(levels, k // 32))).repeat(32)
    a = np.empty((k // 512, 16))
    for p in range(k // 512):
        a[p, :8] = np.random.permutation(np.resize(levels, 8))
        for g in range(8):
            far = levels[np.abs(levels - a[p, g]) >= 10]
            a[p, g + 8] = far[np.random.randint(len(far))]
    return np.exp2(a.ravel()).repeat(32)


def f64(x):
    return np.asarray(x).astype(np.float64)


def striped(idx):
    return np.tile(np.asarray(idx).reshape(-1, 16).T, (8, 1)).astype(np.uint16)


def unstriped(offs):
    return offs[:16].T.reshape(-1).astype(np.int64)


def striped8(idx):
    return np.asarray(idx).reshape(8, -1, 16).transpose(0, 2, 1).reshape(128, -1).astype(np.uint16)


def unstriped8(offs):
    return offs.reshape(8, 16, -1).transpose(0, 2, 1).reshape(8, -1).astype(np.int64)


def pick8(x, idx, run):
    r = np.arange(len(x))
    return x[r[:, None], idx[r % (8 * run) // run]]


E2M1 = np.array([0.0, 0.5, 1.0, 1.5, 2.0, 3.0, 4.0, 6.0, -0.0, -0.5, -1.0, -1.5, -2.0, -3.0, -4.0, -6.0])


def pack_weight(w, fmt):
    k, n = w.shape
    w = f64(np.asarray(w, np.float32).astype(ml_dtypes.bfloat16)).reshape(k // 32, 32, n)
    amax = np.abs(w).max(1)
    if fmt in ("e4m3", "e5m2"):
        byte = np.frexp(amax)[1] - 1 + 127 - (7 if fmt == "e4m3" else 14)
    else:
        mant, ex = np.frexp(amax / 6.0)
        byte = np.where(mant > 0.5, ex, ex - 1) + 127
    byte = np.clip(np.where(amax > 0, byte, 1), 1, 254)
    scaled = (w * np.exp2(127.0 - byte)[:, None, :]).reshape(k, n).astype(np.float32)
    by_word = np.ascontiguousarray(scaled.reshape(k // 512, 128, 4, n).transpose(0, 1, 3, 2))
    if fmt in ("e4m3", "e5m2"):
        words = by_word.astype(ml_dtypes.float8_e4m3fn if fmt == "e4m3" else ml_dtypes.float8_e5m2).view(np.uint8)
    else:
        c = by_word.astype(ml_dtypes.float4_e2m1fn).view(np.uint8) & 0xF
        words = (c[..., 0::2] | (c[..., 1::2] << 4)).reshape(k // 512, 128, 2 * n)
    return np.ascontiguousarray(words), np.ascontiguousarray(byte.astype(np.uint8).reshape(k // 512, 16, n))


def unpack_weight(words, scales, fmt):
    g, _, n = scales.shape
    words = np.ascontiguousarray(words).reshape(g, 128, n, -1)
    if fmt in ("e4m3", "e5m2"):
        vals = words.view(ml_dtypes.float8_e4m3fn if fmt == "e4m3" else ml_dtypes.float8_e5m2).astype(np.float64)
    else:
        nib = np.empty((g, 128, n, 4), np.uint8)
        nib[..., 0::2] = words & 0xF
        nib[..., 1::2] = words >> 4
        vals = E2M1[nib]
    vals = vals * np.repeat(np.exp2(scales.astype(np.float64) - 127.0), 8, axis=1)[..., None]
    return vals.transpose(0, 1, 3, 2).reshape(g * 512, n)


K, F, T, Z, J, R, O, N, E = 512, 512, 1024, 1024, 256, 512, 128, 256, 1024


def setup_inputs():
    n = np.random.standard_normal
    idx = np.random.permutation(T)[:J]
    idx2 = np.random.permutation(Z)[:J]
    idx3 = np.stack([np.random.permutation(J)[:O] for _ in range(8)])
    idx4 = np.stack([np.random.permutation(J)[:O] for _ in range(8)])
    idx5 = np.random.permutation(E)[:O]
    fk = mx_kscale(K)
    fr = mx_kscale(R)
    ff = mx_kscale(F)
    xtp = pack_weight(n((K, T)) / fk[:, None], "e5m2")
    wp = pack_weight(n((K, R)) * 1 / np.sqrt(K) * fk[:, None] * fr, "e2m1")
    xop = pack_weight(n((F, Z)) / ff[:, None], "e4m3")
    w2p = pack_weight(n((F, R)) * 1 / np.sqrt(F) * ff[:, None] * fr, "e2m1")
    wbp = pack_weight(n((R, N)) * 1 / np.sqrt(R) / fr[:, None], "e2m1")
    return {
        "xt_words": xtp[0],
        "xt_scales": xtp[1],
        "w_words": wp[0],
        "w_scales": wp[1],
        "xo_words": xop[0],
        "xo_scales": xop[1],
        "w2_words": w2p[0],
        "w2_scales": w2p[1],
        "sa": (np.random.uniform(0.5, 1.6, (R, 1))).astype(np.float32),
        "sb": (np.random.uniform(0.5, 1.6, (R, 1))).astype(np.float32),
        "wb_words": wbp[0],
        "wb_scales": wbp[1],
        "tz": (np.random.randint(-9, 10, (N, E)).astype(np.float64)).astype(np.float32),
        "so": (np.random.uniform(0.1, 0.3, (N, 1))).astype(np.float32),
        "offs": striped(idx),
        "offs2": striped(idx2),
        "offs3": striped8(idx3),
        "offs4": striped8(idx4),
        "offs5": striped(idx5),
    }


def reference(xt_words, xt_scales, w_words, w_scales, xo_words, xo_scales, w2_words, w2_scales, sa, sb, wb_words, wb_scales, tz, so, offs, offs2, offs3, offs4, offs5):
    idx = unstriped(offs)
    idx2 = unstriped(offs2)
    idx3 = unstriped8(offs3)
    idx4 = unstriped8(offs4)
    idx5 = unstriped(offs5)
    xtu = unpack_weight(xt_words, xt_scales, "e5m2")
    wu = unpack_weight(w_words, w_scales, "e2m1")
    xou = unpack_weight(xo_words, xo_scales, "e4m3")
    w2u = unpack_weight(w2_words, w2_scales, "e2m1")
    wbu = unpack_weight(wb_words, wb_scales, "e2m1")
    xtidxg = xtu[:, idx]
    a = wu.T @ xtidxg
    xoidx2g = xou[:, idx2]
    b = w2u.T @ xoidx2g
    hid = np.maximum(pick8(a, idx3, 64) * f64(sa), pick8(b, idx4, 64) * f64(sb))
    hidq = mxq(hid, 0, "e4m3")
    p = wbu.T @ hidq
    y = np.maximum(p, f64(tz)[:, idx5] * f64(so))
    return y

@@ -1,0 +1,168 @@
+from contextlib import ExitStack
+
+import concourse.mybir as mybir
+
+F32 = mybir.dt.float32
+BF16 = mybir.dt.bfloat16
+I32 = mybir.dt.int32
+U32 = mybir.dt.uint32
+U16 = mybir.dt.uint16
+U8 = mybir.dt.uint8
+E4M3 = mybir.dt.float8_e4m3fn_x4
+E5M2 = mybir.dt.float8_e5m2_x4
+E2M1 = mybir.dt.float4_e2m1fn_x4
+COPY = mybir.ActivationFunctionType.Copy
+MAX = mybir.AluOpType.max
+
+P = 128
+T, J, R, O, N, E = 1024, 256, 512, 128, 256, 1024
+FLOPS = 2 * 512 * (2 * R * J + N * O)
+
+
+def tile_list_groupmeet_twotab_one_stepfloor_kernel(
+    tc, xt_words, xt_scales, w_words, w_scales, xo_words, xo_scales, w2_words, w2_scales,
+    sa, sb, wb_words, wb_scales, tz, so, offs, offs2, offs3, offs4, offs5, out,
+):
+    nc = tc.nc
+    with ExitStack() as ctx:
+        keep = ctx.enter_context(tc.tile_pool(name="keep", bufs=1))
+        psum = ctx.enter_context(tc.psum_pool(name="psum", bufs=1))
+
+        def new(name, shape, dtype):
+            return keep.tile(shape, dtype, name=name, align_bytes=64)
+
+        l1 = new("l1", [P, J // 16], U16)
+        l2 = new("l2", [P, J // 16], U16)
+        l3 = new("l3", [P, O // 16], U16)
+        l4 = new("l4", [P, O // 16], U16)
+        l5 = new("l5", [P, O // 16], U16)
+        xw = new("xw", [P, T], U32)
+        ow = new("ow", [P, T], U32)
+        xs = new("xs", [P, T], U8)
+        os_ = new("os_", [P, T], U8)
+        ww = new("ww", [P, R], U16)
+        w2w = new("w2w", [P, R], U16)
+        wbw = new("wbw", [P, N], U16)
+        wbs = new("wbs", [P, N], U8)
+        sat = new("sat", [P, 4], F32)
+        sbt = new("sbt", [P, 4], F32)
+        sot = new("sot", [P, 2], F32)
+        tzt = [new(f"tz{c}", [P, E], F32) for c in range(2)]
+
+        def words4(src):
+            return src[0].rearrange("p n t -> p (n t)").bitcast(I32)
+
+        def plane(q, dst, src):
+            for k in range(4):
+                q[k].dma_start(out=dst[32 * k : 32 * k + 4, :].bitcast(I32), in_=src[0, 4 * k : 4 * k + 4, :].bitcast(I32))
+
+        def deal16(dst, src):
+            nc.scalar.copy(
+                out=dst[:].rearrange("p (t c i) -> p c t i", t=4, i=8),
+                in_=src[:].rearrange("p (c i t) -> p c t i", t=4, i=8),
+            )
+
+        def deal8(eng, dst, src):
+            eng.tensor_copy(
+                out=dst.rearrange("p (t c i) -> p c t i", t=4, i=16),
+                in_=src.rearrange("p (c i t) -> p c t i", t=4, i=16),
+            )
+
+        S, A, G = nc.sync, nc.scalar, nc.gpsimd
+        wp = new("wp", [P, R], U16)
+        w2p = new("w2p", [P, R], U16)
+        wsp = new("wsp", [P, R], U8)
+        w2sp = new("w2sp", [P, R], U8)
+        xg = new("xg", [P, J], U32)
+        og = new("og", [P, J], U32)
+        xsg = new("xsg", [P, J], U8)
+        osg = new("osg", [P, J], U8)
+        ga = new("ga", [P, 4, O], F32)
+        gb = new("gb", [P, 4, O], F32)
+        hb = new("hb", [P, O, 4], BF16)
+        hq = new("hq", [P, O], U32)
+        hs = new("hs", [P, O], U8)
+        av = [new(f"av{t}", [P, J], F32) for t in range(4)]
+        bv = [new(f"bv{t}", [P, J], F32) for t in range(4)]
+        res = [new(f"res{c}", [P, O], F32) for c in range(2)]
+
+        wsc = new("wsc", [P, 2, R], U8)
+        wst = new("wst", [4, 4, 2, R // 4], I32)
+        xst = new("xst", [4, 4, T // 4], I32)
+        for pl in (xs, os_, wbs):
+            nc.vector.memset(pl[:].bitcast(I32), 0)
+        nc.vector.memset(wsc[:].rearrange("p a n -> p (a n)").bitcast(I32), 0)
+
+        def stage(q, dst, src):
+            q.dma_start(out=dst, in_=src[0].bitcast(I32).rearrange("(q r) n -> r q n", r=4))
+
+        def spread(dst, src):
+            for q in range(4):
+                nc.vector.tensor_copy(out=dst[32 * q : 32 * q + 4, :], in_=src[:, q])
+
+        stage(A, xst[:], xt_scales)
+        S.dma_start(out=l1[:], in_=offs)
+        stage(A, wst[:, :, 0, :], w_scales)
+        stage(A, wst[:, :, 1, :], w2_scales)
+        S.dma_start(out=ww[:].bitcast(I32), in_=w_words[0].bitcast(I32))
+        S.dma_start(out=xw[:].bitcast(I32), in_=words4(xt_words))
+        S.dma_start(out=w2w[:].bitcast(I32), in_=w2_words[0].bitcast(I32))
+        S.dma_start(out=l3[:], in_=offs3)
+        S.dma_start(out=ow[:].bitcast(I32), in_=words4(xo_words))
+        S.dma_start(out=l2[:], in_=offs2)
+        plane((S, S, S, S), os_, xo_scales)
+        G.dma_start(out=sat[:], in_=sa.rearrange("(p t) o -> p (t o)", t=4))
+        G.dma_start(out=sbt[:], in_=sb.rearrange("(p t) o -> p (t o)", t=4))
+        S.dma_start(out=l4[:], in_=offs4)
+        for c in range(2):
+            S.dma_start(out=tzt[c][:], in_=tz[P * c : P * (c + 1), :])
+        S.dma_start(out=l5[:], in_=offs5)
+        S.dma_start(out=wbw[:].bitcast(I32), in_=wb_words[0].bitcast(I32))
+        with nc.allow_non_contiguous_dma(reason="one step a partition and half"):
+            G.dma_start(out=sot[:], in_=so.rearrange("(c p) o -> p (c o)", c=2))
+        plane((S, S, S, S), wbs, wb_scales)
+
+        deal16(wp, ww)
+        deal16(w2p, w2w)
+        spread(xs[:].bitcast(I32), xst)
+        nc.vector.tensor_copy(out=xsg[:], in_=xs[:].indirect(l1[:]))
+        spread(wsc[:].rearrange("p a n -> p (a n)").bitcast(I32), wst[:].rearrange("r q a n -> r q (a n)"))
+        deal8(nc.vector, wsp[:], wsc[:, 0, :])
+        nc.vector.tensor_copy(out=xg[:], in_=xw[:].indirect(l1[:]))
+        pa = [psum.tile([P, J], F32, name=f"pa{t}", tag=f"bank{t}") for t in range(4)]
+        for t in range(4):
+            nc.tensor.matmul_mx(out=pa[t][:], lhsT=wp[:, P * t : P * (t + 1)].bitcast(E2M1), lhsT_scale=wsp[:, P * t : P * (t + 1)],
+                                rhs=xg[:].bitcast(E5M2), rhs_scale=xsg[:], start=True, stop=True)
+        nc.vector.tensor_copy(out=osg[:], in_=os_[:].indirect(l2[:]))
+        deal8(nc.vector, w2sp[:], wsc[:, 1, :])
+        nc.vector.tensor_copy(out=og[:], in_=ow[:].indirect(l2[:]))
+        pb = [psum.tile([P, J], F32, name=f"pb{t}", tag=f"bank{4 + t}") for t in range(4)]
+        for t in range(4):
+            nc.tensor.matmul_mx(out=pb[t][:], lhsT=w2p[:, P * t : P * (t + 1)].bitcast(E2M1), lhsT_scale=w2sp[:, P * t : P * (t + 1)],
+                                rhs=og[:].bitcast(E4M3), rhs_scale=osg[:], start=True, stop=True)
+        for t in range(4):
+            if t < 3:
+                nc.scalar.activation(out=av[t][:], in_=pa[t][:], func=COPY)
+            else:
+                nc.vector.tensor_copy(out=av[t][:], in_=pa[t][:])
+            nc.scalar.activation(out=ga[:, t, :], in_=av[t][:].indirect(l3[:]), func=COPY, scale=sat[:, t : t + 1])
+        for t in range(4):
+            nc.vector.tensor_copy(out=bv[t][:], in_=pb[t][:])
+            nc.scalar.activation(out=gb[:, t, :], in_=bv[t][:].indirect(l4[:]), func=COPY, scale=sbt[:, t : t + 1])
+        gz = keep.tile([P, 2, O], F32, name="gz", tag="bv3", align_bytes=64)
+        for c in range(2):
+            nc.scalar.activation(out=gz[:, c, :], in_=tzt[c][:].indirect(l5[:]), func=COPY, scale=sot[:, c : c + 1])
+        for u in range(2):
+            nc.vector.tensor_tensor(
+                out=hb[:, :, 2 * u : 2 * u + 2].rearrange("p (c i) t -> p c t i", i=4),
+                in0=ga[:, 2 * u : 2 * u + 2, :].rearrange("p t (c i) -> p c t i", i=4),
+                in1=gb[:, 2 * u : 2 * u + 2, :].rearrange("p t (c i) -> p c t i", i=4),
+                op=MAX,
+            )
+        nc.vector.quantize_mx(out=hq[:].bitcast(E4M3), scales=hs[:], in_=hb[:].rearrange("p o t -> p (o t)"))
+        for c in range(2):
+            pp = psum.tile([P, O], F32, name=f"pp{c}", tag=f"bank{c}")
+            nc.tensor.matmul_mx(out=pp[:], lhsT=wbw[:, P * c : P * (c + 1)].bitcast(E2M1), lhsT_scale=wbs[:, P * c : P * (c + 1)],
+                                rhs=hq[:].bitcast(E4M3), rhs_scale=hs[:], start=True, stop=True)
+            nc.vector.tensor_tensor(out=res[c][:], in0=pp[:], in1=gz[:, c, :], op=MAX)
+            (S, A)[c].dma_start(out=out[P * c : P * (c + 1), :], in_=res[c][:])

@@ -37,13 +37,13 @@ def tile_list_groupmeet_twotab_one_stepfloor_kernel(
         l4 = new("l4", [P, O // 16], U16)
         l5 = new("l5", [P, O // 16], U16)
         xw = new("xw", [P, T], U32)
-        ow = new("ow", [P, T], U32)
+        reuse = ctx.enter_context(tc.tile_pool(name="reuse", bufs=1))
+        ow = reuse.tile([P, T], U32, name="ow", align_bytes=64, offset=0)
+        os_ = reuse.tile([P, T], U8, name="os_", align_bytes=64, offset=4096)
         xs = new("xs", [P, T], U8)
-        os_ = new("os_", [P, T], U8)
         ww = new("ww", [P, R], U16)
         w2w = new("w2w", [P, R], U16)
         wbw = new("wbw", [P, N], U16)
-        wbs = new("wbs", [P, N], U8)
         sat = new("sat", [P, 4], F32)
         sbt = new("sbt", [P, 4], F32)
         sot = new("sot", [P, 2], F32)
@@ -82,84 +82,88 @@ def tile_list_groupmeet_twotab_one_stepfloor_kernel(
         hb = new("hb", [P, O, 4], BF16)
         hq = new("hq", [P, O], U32)
         hs = new("hs", [P, O], U8)
-        av = [new(f"av{t}", [P, J], F32) for t in range(4)]
+        av = [new(f"av{t}", [P, J], F32) for t in range(2)] + [0, 0]
         bv = [new(f"bv{t}", [P, J], F32) for t in range(4)]
         res = [new(f"res{c}", [P, O], F32) for c in range(2)]
 
-        wsc = new("wsc", [P, 2, R], U8)
-        wst = new("wst", [4, 4, 2, R // 4], I32)
+        wsc = new("wsc", [P, 2 * R + N], U8)
+        wst = new("wst", [4, 4, (2 * R + N) // 4], I32)
         xst = new("xst", [4, 4, T // 4], I32)
-        for pl in (xs, os_, wbs):
+        for pl in (wsc, xs, os_):
             nc.vector.memset(pl[:].bitcast(I32), 0)
-        nc.vector.memset(wsc[:].rearrange("p a n -> p (a n)").bitcast(I32), 0)
+        wbs = wsc[:, 2 * R :]
 
         def stage(q, dst, src):
             q.dma_start(out=dst, in_=src[0].bitcast(I32).rearrange("(q r) n -> r q n", r=4))
 
         def spread(dst, src):
             for q in range(4):
-                nc.vector.tensor_copy(out=dst[32 * q : 32 * q + 4, :], in_=src[:, q])
+                nc.vector.tensor_copy(out=dst[32 * q : 32 * q + 4, :].bitcast(I32), in_=src[:, q])
 
+        stage(S, wst[:, :, 0 : R // 4], w_scales)
+        stage(A, wst[:, :, R // 4 : R // 2], w2_scales)
+        stage(S, wst[:, :, R // 2 :], wb_scales)
         stage(A, xst[:], xt_scales)
         S.dma_start(out=l1[:], in_=offs)
-        stage(A, wst[:, :, 0, :], w_scales)
-        stage(A, wst[:, :, 1, :], w2_scales)
         S.dma_start(out=ww[:].bitcast(I32), in_=w_words[0].bitcast(I32))
-        S.dma_start(out=xw[:].bitcast(I32), in_=words4(xt_words))
+        A.dma_start(out=xw[:].bitcast(I32), in_=words4(xt_words))
         S.dma_start(out=w2w[:].bitcast(I32), in_=w2_words[0].bitcast(I32))
-        S.dma_start(out=l3[:], in_=offs3)
         S.dma_start(out=ow[:].bitcast(I32), in_=words4(xo_words))
         S.dma_start(out=l2[:], in_=offs2)
-        plane((S, S, S, S), os_, xo_scales)
-        G.dma_start(out=sat[:], in_=sa.rearrange("(p t) o -> p (t o)", t=4))
-        G.dma_start(out=sbt[:], in_=sb.rearrange("(p t) o -> p (t o)", t=4))
+        plane([S] * 4, os_, xo_scales)
+        S.dma_start(out=l3[:], in_=offs3)
+        S.dma_start(out=sat[:], in_=sa.rearrange("(p t) o -> p (t o)", t=4))
         S.dma_start(out=l4[:], in_=offs4)
-        for c in range(2):
-            S.dma_start(out=tzt[c][:], in_=tz[P * c : P * (c + 1), :])
+        S.dma_start(out=sbt[:], in_=sb.rearrange("(p t) o -> p (t o)", t=4))
+        S.dma_start(out=tzt[0][:], in_=tz[0:P, :])
+        S.dma_start(out=tzt[1][:], in_=tz[P : 2 * P, :])
         S.dma_start(out=l5[:], in_=offs5)
-        S.dma_start(out=wbw[:].bitcast(I32), in_=wb_words[0].bitcast(I32))
         with nc.allow_non_contiguous_dma(reason="one step a partition and half"):
-            G.dma_start(out=sot[:], in_=so.rearrange("(c p) o -> p (c o)", c=2))
-        plane((S, S, S, S), wbs, wb_scales)
+            S.dma_start(out=sot[:], in_=so.rearrange("(c p) o -> p (c o)", c=2))
+        S.dma_start(out=wbw[:].bitcast(I32), in_=wb_words[0].bitcast(I32))
 
         deal16(wp, ww)
         deal16(w2p, w2w)
-        spread(xs[:].bitcast(I32), xst)
+        spread(wsc, wst)
+        deal8(G, wsp[:], wsc[:, 0:R])
+        spread(xs, xst)
         nc.vector.tensor_copy(out=xsg[:], in_=xs[:].indirect(l1[:]))
-        spread(wsc[:].rearrange("p a n -> p (a n)").bitcast(I32), wst[:].rearrange("r q a n -> r q (a n)"))
-        deal8(nc.vector, wsp[:], wsc[:, 0, :])
         nc.vector.tensor_copy(out=xg[:], in_=xw[:].indirect(l1[:]))
         pa = [psum.tile([P, J], F32, name=f"pa{t}", tag=f"bank{t}") for t in range(4)]
         for t in range(4):
             nc.tensor.matmul_mx(out=pa[t][:], lhsT=wp[:, P * t : P * (t + 1)].bitcast(E2M1), lhsT_scale=wsp[:, P * t : P * (t + 1)],
                                 rhs=xg[:].bitcast(E5M2), rhs_scale=xsg[:], start=True, stop=True)
+        deal8(G, w2sp[:], wsc[:, R : 2 * R])
         nc.vector.tensor_copy(out=osg[:], in_=os_[:].indirect(l2[:]))
-        deal8(nc.vector, w2sp[:], wsc[:, 1, :])
         nc.vector.tensor_copy(out=og[:], in_=ow[:].indirect(l2[:]))
         pb = [psum.tile([P, J], F32, name=f"pb{t}", tag=f"bank{4 + t}") for t in range(4)]
         for t in range(4):
             nc.tensor.matmul_mx(out=pb[t][:], lhsT=w2p[:, P * t : P * (t + 1)].bitcast(E2M1), lhsT_scale=w2sp[:, P * t : P * (t + 1)],
                                 rhs=og[:].bitcast(E4M3), rhs_scale=osg[:], start=True, stop=True)
+        av[3] = reuse.tile([P, J], F32, name="av3", align_bytes=64, offset=4608)
+        av[2] = reuse.tile([P, J], F32, name="av2", align_bytes=64, offset=3584)
         for t in range(4):
-            if t < 3:
+            if t < 2:
                 nc.scalar.activation(out=av[t][:], in_=pa[t][:], func=COPY)
             else:
                 nc.vector.tensor_copy(out=av[t][:], in_=pa[t][:])
             nc.scalar.activation(out=ga[:, t, :], in_=av[t][:].indirect(l3[:]), func=COPY, scale=sat[:, t : t + 1])
         for t in range(4):
             nc.vector.tensor_copy(out=bv[t][:], in_=pb[t][:])
-            nc.scalar.activation(out=gb[:, t, :], in_=bv[t][:].indirect(l4[:]), func=COPY, scale=sbt[:, t : t + 1])
+            for lo, hi in ((0, O),) if t < 3 else ((0, O // 2), (O // 2, O)):
+                nc.scalar.activation(out=gb[:, t, lo:hi], in_=bv[t][:].indirect(l4[:, lo // 16 : hi // 16]), func=COPY, scale=sbt[:, t : t + 1])
         gz = keep.tile([P, 2, O], F32, name="gz", tag="bv3", align_bytes=64)
         for c in range(2):
             nc.scalar.activation(out=gz[:, c, :], in_=tzt[c][:].indirect(l5[:]), func=COPY, scale=sot[:, c : c + 1])
-        for u in range(2):
+        for u, lo, hi in ((0, 0, O), (1, 0, O // 2), (1, O // 2, O)):
             nc.vector.tensor_tensor(
-                out=hb[:, :, 2 * u : 2 * u + 2].rearrange("p (c i) t -> p c t i", i=4),
-                in0=ga[:, 2 * u : 2 * u + 2, :].rearrange("p t (c i) -> p c t i", i=4),
-                in1=gb[:, 2 * u : 2 * u + 2, :].rearrange("p t (c i) -> p c t i", i=4),
+                out=hb[:, lo:hi, 2 * u : 2 * u + 2].rearrange("p (c i) t -> p c t i", i=4),
+                in0=ga[:, 2 * u : 2 * u + 2, lo:hi].rearrange("p t (c i) -> p c t i", i=4),
+                in1=gb[:, 2 * u : 2 * u + 2, lo:hi].rearrange("p t (c i) -> p c t i", i=4),
                 op=MAX,
             )
-        nc.vector.quantize_mx(out=hq[:].bitcast(E4M3), scales=hs[:], in_=hb[:].rearrange("p o t -> p (o t)"))
+        for lo, hi in ((0, O // 2), (O // 2, O)):
+            nc.vector.quantize_mx(out=hq[:, lo:hi].bitcast(E4M3), scales=hs[:, lo:hi], in_=hb[:, lo:hi, :].rearrange("p o t -> p (o t)"))
         for c in range(2):
             pp = psum.tile([P, O], F32, name=f"pp{c}", tag=f"bank{c}")
             nc.tensor.matmul_mx(out=pp[:], lhsT=wbw[:, P * c : P * (c + 1)].bitcast(E2M1), lhsT_scale=wbs[:, P * c : P * (c + 1)],

@@ -108,24 +108,24 @@ def tile_list_groupmeet_twotab_one_stepfloor_kernel(
         S.dma_start(out=ww[:].bitcast(I32), in_=w_words[0].bitcast(I32))
         A.dma_start(out=xw[:].bitcast(I32), in_=words4(xt_words))
         S.dma_start(out=w2w[:].bitcast(I32), in_=w2_words[0].bitcast(I32))
+        G.dma_start(out=sat[:], in_=sa.rearrange("(p t) o -> p (t o)", t=4))
+        G.dma_start(out=sbt[:], in_=sb.rearrange("(p t) o -> p (t o)", t=4))
+        with nc.allow_non_contiguous_dma(reason="one step a partition and half"):
+            G.dma_start(out=sot[:], in_=so.rearrange("(c p) o -> p (c o)", c=2))
         S.dma_start(out=ow[:].bitcast(I32), in_=words4(xo_words))
         S.dma_start(out=l2[:], in_=offs2)
         plane([S] * 4, os_, xo_scales)
         S.dma_start(out=l3[:], in_=offs3)
-        S.dma_start(out=sat[:], in_=sa.rearrange("(p t) o -> p (t o)", t=4))
-        S.dma_start(out=l4[:], in_=offs4)
-        S.dma_start(out=sbt[:], in_=sb.rearrange("(p t) o -> p (t o)", t=4))
         S.dma_start(out=tzt[0][:], in_=tz[0:P, :])
+        S.dma_start(out=l4[:], in_=offs4)
         S.dma_start(out=tzt[1][:], in_=tz[P : 2 * P, :])
         S.dma_start(out=l5[:], in_=offs5)
-        with nc.allow_non_contiguous_dma(reason="one step a partition and half"):
-            S.dma_start(out=sot[:], in_=so.rearrange("(c p) o -> p (c o)", c=2))
         S.dma_start(out=wbw[:].bitcast(I32), in_=wb_words[0].bitcast(I32))
 
         deal16(wp, ww)
         deal16(w2p, w2w)
         spread(wsc, wst)
-        deal8(G, wsp[:], wsc[:, 0:R])
+        deal8(nc.vector, wsp[:], wsc[:, 0:R])
         spread(xs, xst)
         nc.vector.tensor_copy(out=xsg[:], in_=xs[:].indirect(l1[:]))
         nc.vector.tensor_copy(out=xg[:], in_=xw[:].indirect(l1[:]))
@@ -133,7 +133,7 @@ def tile_list_groupmeet_twotab_one_stepfloor_kernel(
         for t in range(4):
             nc.tensor.matmul_mx(out=pa[t][:], lhsT=wp[:, P * t : P * (t + 1)].bitcast(E2M1), lhsT_scale=wsp[:, P * t : P * (t + 1)],
                                 rhs=xg[:].bitcast(E5M2), rhs_scale=xsg[:], start=True, stop=True)
-        deal8(G, w2sp[:], wsc[:, R : 2 * R])
+        deal8(nc.vector, w2sp[:], wsc[:, R : 2 * R])
         nc.vector.tensor_copy(out=osg[:], in_=os_[:].indirect(l2[:]))
         nc.vector.tensor_copy(out=og[:], in_=ow[:].indirect(l2[:]))
         pb = [psum.tile([P, J], F32, name=f"pb{t}", tag=f"bank{4 + t}") for t in range(4)]

@@ -44,6 +44,7 @@ def tile_list_groupmeet_twotab_one_stepfloor_kernel(
         ww = new("ww", [P, R], U16)
         w2w = new("w2w", [P, R], U16)
         wbw = new("wbw", [P, N], U16)
+        wbs = new("wbs", [P, N], U8)
         sat = new("sat", [P, 4], F32)
         sbt = new("sbt", [P, 4], F32)
         sot = new("sot", [P, 2], F32)
@@ -86,12 +87,11 @@ def tile_list_groupmeet_twotab_one_stepfloor_kernel(
         bv = [new(f"bv{t}", [P, J], F32) for t in range(4)]
         res = [new(f"res{c}", [P, O], F32) for c in range(2)]
 
-        wsc = new("wsc", [P, 2 * R + N], U8)
-        wst = new("wst", [4, 4, (2 * R + N) // 4], I32)
+        wsc = new("wsc", [P, 2 * R], U8)
+        wst = new("wst", [4, 4, 2 * R // 4], I32)
         xst = new("xst", [4, 4, T // 4], I32)
-        for pl in (wsc, xs, os_):
+        for pl in (wsc, xs, os_, wbs):
             nc.vector.memset(pl[:].bitcast(I32), 0)
-        wbs = wsc[:, 2 * R :]
 
         def stage(q, dst, src):
             q.dma_start(out=dst, in_=src[0].bitcast(I32).rearrange("(q r) n -> r q n", r=4))
@@ -102,7 +102,6 @@ def tile_list_groupmeet_twotab_one_stepfloor_kernel(
 
         stage(S, wst[:, :, 0 : R // 4], w_scales)
         stage(A, wst[:, :, R // 4 : R // 2], w2_scales)
-        stage(S, wst[:, :, R // 2 :], wb_scales)
         stage(A, xst[:], xt_scales)
         S.dma_start(out=l1[:], in_=offs)
         S.dma_start(out=ww[:].bitcast(I32), in_=w_words[0].bitcast(I32))
@@ -116,8 +115,9 @@ def tile_list_groupmeet_twotab_one_stepfloor_kernel(
         S.dma_start(out=l2[:], in_=offs2)
         plane([S] * 4, os_, xo_scales)
         S.dma_start(out=l3[:], in_=offs3)
-        S.dma_start(out=tzt[0][:], in_=tz[0:P, :])
         S.dma_start(out=l4[:], in_=offs4)
+        S.dma_start(out=tzt[0][:], in_=tz[0:P, :])
+        plane([S] * 4, wbs, wb_scales)
         S.dma_start(out=tzt[1][:], in_=tz[P : 2 * P, :])
         S.dma_start(out=l5[:], in_=offs5)
         S.dma_start(out=wbw[:].bitcast(I32), in_=wb_words[0].bitcast(I32))

@@ -15,8 +15,19 @@ COPY = mybir.ActivationFunctionType.Copy
 MAX = mybir.AluOpType.max
 
 P = 128
+PACK = 4
+QUADS = 4
+QUAD = P // QUADS
+ROWS = 4
+STRIPE = 16
+LINE = 16
+WORD = 4
+K = 512
 T, J, R, O, N, E = 1024, 256, 512, 128, 256, 1024
-FLOPS = 2 * 512 * (2 * R * J + N * O)
+HALVES = ((0, O // 2), (O // 2, O))
+OUT_TILES = N // P
+A_ON_SCALAR = 2
+FLOPS = 2 * K * (2 * R * J + N * O)
 
 
 def tile_list_groupmeet_twotab_one_stepfloor_kernel(
@@ -31,142 +42,170 @@ def tile_list_groupmeet_twotab_one_stepfloor_kernel(
         def new(name, shape, dtype):
             return keep.tile(shape, dtype, name=name, align_bytes=64)
 
-        l1 = new("l1", [P, J // 16], U16)
-        l2 = new("l2", [P, J // 16], U16)
-        l3 = new("l3", [P, O // 16], U16)
-        l4 = new("l4", [P, O // 16], U16)
-        l5 = new("l5", [P, O // 16], U16)
-        xw = new("xw", [P, T], U32)
+        token_list = new("token_list", [P, J // STRIPE], U16)
+        note_list = new("note_list", [P, J // STRIPE], U16)
+        a_lists = new("a_lists", [P, O // STRIPE], U16)
+        b_lists = new("b_lists", [P, O // STRIPE], U16)
+        entry_list = new("entry_list", [P, O // STRIPE], U16)
+        xt_table = new("xt_table", [P, T], U32)
         reuse = ctx.enter_context(tc.tile_pool(name="reuse", bufs=1))
-        ow = reuse.tile([P, T], U32, name="ow", align_bytes=64, offset=0)
-        os_ = reuse.tile([P, T], U8, name="os_", align_bytes=64, offset=4096)
-        xs = new("xs", [P, T], U8)
-        ww = new("ww", [P, R], U16)
-        w2w = new("w2w", [P, R], U16)
-        wbw = new("wbw", [P, N], U16)
-        wbs = new("wbs", [P, N], U8)
-        sat = new("sat", [P, 4], F32)
-        sbt = new("sbt", [P, 4], F32)
-        sot = new("sot", [P, 2], F32)
-        tzt = [new(f"tz{c}", [P, E], F32) for c in range(2)]
+        xo_table_bytes = T * WORD
+        xo_table = reuse.tile([P, T], U32, name="xo_table", align_bytes=64, offset=0)
+        xo_plane = reuse.tile([P, T], U8, name="xo_plane", align_bytes=64, offset=xo_table_bytes)
+        xt_plane = new("xt_plane", [P, T], U8)
+        w_loaded = new("w_loaded", [P, R], U16)
+        w2_loaded = new("w2_loaded", [P, R], U16)
+        wb_loaded = new("wb_loaded", [P, N], U16)
+        wb_plane = new("wb_plane", [P, N], U8)
+        sa_cols = new("sa_cols", [P, PACK], F32)
+        sb_cols = new("sb_cols", [P, PACK], F32)
+        so_cols = new("so_cols", [P, OUT_TILES], F32)
+        tz_rows = [new(f"tz_rows{c}", [P, E], F32) for c in range(OUT_TILES)]
+        w_dealt = new("w_dealt", [P, R], U16)
+        w2_dealt = new("w2_dealt", [P, R], U16)
+        w_plane_dealt = new("w_plane_dealt", [P, R], U8)
+        w2_plane_dealt = new("w2_plane_dealt", [P, R], U8)
+        xt_picked = new("xt_picked", [P, J], U32)
+        xo_picked = new("xo_picked", [P, J], U32)
+        xt_plane_picked = new("xt_plane_picked", [P, J], U8)
+        xo_plane_picked = new("xo_plane_picked", [P, J], U8)
+        a_scaled = new("a_scaled", [P, PACK, O], F32)
+        b_scaled = new("b_scaled", [P, PACK, O], F32)
+        hid = new("hid", [P, O, PACK], BF16)
+        hid_words = new("hid_words", [P, O], U32)
+        hid_plane = new("hid_plane", [P, O], U8)
+        a_rows = [new(f"a_rows{t}", [P, J], F32) for t in range(A_ON_SCALAR)]
+        b_rows = [new(f"b_rows{t}", [P, J], F32) for t in range(PACK)]
+        result = [new(f"result{c}", [P, O], F32) for c in range(OUT_TILES)]
+        w_planes = new("w_planes", [P, 2 * R], U8)
+        w_stage = new("w_stage", [ROWS, QUADS, 2 * R // WORD], I32)
+        xt_stage = new("xt_stage", [P // 2 + ROWS, 2, T // WORD], I32)
 
-        def words4(src):
-            return src[0].rearrange("p n t -> p (n t)").bitcast(I32)
+        for plane in (xt_plane, w_planes, xo_plane, wb_plane):
+            nc.vector.memset(plane[:].bitcast(I32), 0)
 
-        def plane(q, dst, src):
-            for k in range(4):
-                q[k].dma_start(out=dst[32 * k : 32 * k + 4, :].bitcast(I32), in_=src[0, 4 * k : 4 * k + 4, :].bitcast(I32))
+        def load_fp8_words(dst, src):
+            nc.sync.dma_start(out=dst[:].bitcast(I32), in_=src[0].rearrange("p n t -> p (n t)").bitcast(I32))
 
-        def deal16(dst, src):
-            nc.scalar.copy(
-                out=dst[:].rearrange("p (t c i) -> p c t i", t=4, i=8),
-                in_=src[:].rearrange("p (c i t) -> p c t i", t=4, i=8),
+        def load_fp4_words(dst, src):
+            nc.sync.dma_start(out=dst[:].bitcast(I32), in_=src[0].bitcast(I32))
+
+        def load_plane(dst, src):
+            for q in range(QUADS):
+                nc.sync.dma_start(
+                    out=dst[QUAD * q : QUAD * q + ROWS, :].bitcast(I32),
+                    in_=src[0, ROWS * q : ROWS * (q + 1), :].bitcast(I32),
+                )
+
+        def stage(queue, dst, rows):
+            queue.dma_start(out=dst, in_=rows.bitcast(I32).rearrange("(q r) n -> r q n", r=ROWS))
+
+        def deal(copy, dst, src, run):
+            copy(
+                out=dst.rearrange("p (t c i) -> p c t i", t=PACK, i=run),
+                in_=src.rearrange("p (c i t) -> p c t i", t=PACK, i=run),
             )
 
-        def deal8(eng, dst, src):
-            eng.tensor_copy(
-                out=dst.rearrange("p (t c i) -> p c t i", t=4, i=16),
-                in_=src.rearrange("p (c i t) -> p c t i", t=4, i=16),
+        def products(banks, words, plane, picked, picked_plane):
+            for t in range(PACK):
+                cols = slice(P * t, P * (t + 1))
+                nc.tensor.matmul_mx(
+                    out=banks[t][:], lhsT=words[:, cols].bitcast(E2M1), lhsT_scale=plane[:, cols],
+                    rhs=picked, rhs_scale=picked_plane[:], start=True, stop=True,
+                )
+
+        for h, queue in enumerate((nc.sync, nc.scalar)):
+            stage(queue, xt_stage[P // 2 * h : P // 2 * h + ROWS], xt_scales[0, 2 * ROWS * h : 2 * ROWS * (h + 1)])
+        stage(nc.sync, w_stage[:, :, 0 : R // WORD], w_scales[0])
+        stage(nc.scalar, w_stage[:, :, R // WORD :], w2_scales[0])
+        nc.sync.dma_start(out=token_list[:], in_=offs)
+        load_fp4_words(w_loaded, w_words)
+        load_fp8_words(xt_table, xt_words)
+        load_fp4_words(w2_loaded, w2_words)
+        nc.gpsimd.dma_start(out=sa_cols[:], in_=sa.rearrange("(p t) o -> p (t o)", t=PACK))
+        nc.gpsimd.dma_start(out=sb_cols[:], in_=sb.rearrange("(p t) o -> p (t o)", t=PACK))
+        with nc.allow_non_contiguous_dma(reason="one step for each partition and output tile"):
+            nc.gpsimd.dma_start(out=so_cols[:], in_=so.rearrange("(c p) o -> p (c o)", c=OUT_TILES))
+        load_fp8_words(xo_table, xo_words)
+        nc.sync.dma_start(out=note_list[:], in_=offs2)
+        load_plane(xo_plane, xo_scales)
+        nc.sync.dma_start(out=a_lists[:], in_=offs3)
+        nc.sync.dma_start(out=b_lists[:], in_=offs4)
+        nc.sync.dma_start(out=tz_rows[0][:], in_=tz[0:P, :])
+        load_plane(wb_plane, wb_scales)
+        nc.sync.dma_start(out=tz_rows[1][:], in_=tz[P : 2 * P, :])
+        nc.sync.dma_start(out=entry_list[:], in_=offs5)
+        load_fp4_words(wb_loaded, wb_words)
+
+        deal(nc.scalar.copy, w_dealt[:], w_loaded[:], LINE // 2)
+        deal(nc.scalar.copy, w2_dealt[:], w2_loaded[:], LINE // 2)
+        for q in range(QUADS):
+            h, s = divmod(q, 2)
+            nc.vector.tensor_copy(
+                out=xt_plane[QUAD * q : QUAD * q + ROWS, :].bitcast(I32),
+                in_=xt_stage[P // 2 * h : P // 2 * h + ROWS, s],
             )
+        for q in range(QUADS):
+            nc.vector.tensor_copy(out=w_planes[QUAD * q : QUAD * q + ROWS, :].bitcast(I32), in_=w_stage[:, q])
+        nc.vector.tensor_copy(out=xt_plane_picked[:], in_=xt_plane[:].indirect(token_list[:]))
+        deal(nc.vector.tensor_copy, w_plane_dealt[:], w_planes[:, 0:R], LINE)
+        nc.vector.tensor_copy(out=xt_picked[:], in_=xt_table[:].indirect(token_list[:]))
+        a_banks = [psum.tile([P, J], F32, name=f"a_bank{t}", tag=f"bank{t}") for t in range(PACK)]
+        products(a_banks, w_dealt, w_plane_dealt, xt_picked[:].bitcast(E5M2), xt_plane_picked)
 
-        S, A, G = nc.sync, nc.scalar, nc.gpsimd
-        wp = new("wp", [P, R], U16)
-        w2p = new("w2p", [P, R], U16)
-        wsp = new("wsp", [P, R], U8)
-        w2sp = new("w2sp", [P, R], U8)
-        xg = new("xg", [P, J], U32)
-        og = new("og", [P, J], U32)
-        xsg = new("xsg", [P, J], U8)
-        osg = new("osg", [P, J], U8)
-        ga = new("ga", [P, 4, O], F32)
-        gb = new("gb", [P, 4, O], F32)
-        hb = new("hb", [P, O, 4], BF16)
-        hq = new("hq", [P, O], U32)
-        hs = new("hs", [P, O], U8)
-        av = [new(f"av{t}", [P, J], F32) for t in range(2)] + [0, 0]
-        bv = [new(f"bv{t}", [P, J], F32) for t in range(4)]
-        res = [new(f"res{c}", [P, O], F32) for c in range(2)]
+        deal(nc.vector.tensor_copy, w2_plane_dealt[:], w_planes[:, R : 2 * R], LINE)
+        nc.vector.tensor_copy(out=xo_plane_picked[:], in_=xo_plane[:].indirect(note_list[:]))
+        nc.vector.tensor_copy(out=xo_picked[:], in_=xo_table[:].indirect(note_list[:]))
+        b_banks = [psum.tile([P, J], F32, name=f"b_bank{t}", tag=f"bank{PACK + t}") for t in range(PACK)]
+        products(b_banks, w2_dealt, w2_plane_dealt, xo_picked[:].bitcast(E4M3), xo_plane_picked)
 
-        wsc = new("wsc", [P, 2 * R], U8)
-        wst = new("wst", [4, 4, 2 * R // 4], I32)
-        xst = new("xst", [4, 4, T // 4], I32)
-        for pl in (wsc, xs, os_, wbs):
-            nc.vector.memset(pl[:].bitcast(I32), 0)
+        first_offset = xo_table_bytes - T // 2
+        last_a = reuse.tile([P, J], F32, name="a_rows3", align_bytes=64, offset=first_offset + J * WORD)
+        third_a = reuse.tile([P, J], F32, name="a_rows2", align_bytes=64, offset=first_offset)
+        a_rows.extend([third_a, last_a])
 
-        def stage(q, dst, src):
-            q.dma_start(out=dst, in_=src[0].bitcast(I32).rearrange("(q r) n -> r q n", r=4))
-
-        def spread(dst, src):
-            for q in range(4):
-                nc.vector.tensor_copy(out=dst[32 * q : 32 * q + 4, :].bitcast(I32), in_=src[:, q])
-
-        stage(S, wst[:, :, 0 : R // 4], w_scales)
-        stage(A, wst[:, :, R // 4 : R // 2], w2_scales)
-        stage(A, xst[:], xt_scales)
-        S.dma_start(out=l1[:], in_=offs)
-        S.dma_start(out=ww[:].bitcast(I32), in_=w_words[0].bitcast(I32))
-        A.dma_start(out=xw[:].bitcast(I32), in_=words4(xt_words))
-        S.dma_start(out=w2w[:].bitcast(I32), in_=w2_words[0].bitcast(I32))
-        G.dma_start(out=sat[:], in_=sa.rearrange("(p t) o -> p (t o)", t=4))
-        G.dma_start(out=sbt[:], in_=sb.rearrange("(p t) o -> p (t o)", t=4))
-        with nc.allow_non_contiguous_dma(reason="one step a partition and half"):
-            G.dma_start(out=sot[:], in_=so.rearrange("(c p) o -> p (c o)", c=2))
-        S.dma_start(out=ow[:].bitcast(I32), in_=words4(xo_words))
-        S.dma_start(out=l2[:], in_=offs2)
-        plane([S] * 4, os_, xo_scales)
-        S.dma_start(out=l3[:], in_=offs3)
-        S.dma_start(out=l4[:], in_=offs4)
-        S.dma_start(out=tzt[0][:], in_=tz[0:P, :])
-        plane([S] * 4, wbs, wb_scales)
-        S.dma_start(out=tzt[1][:], in_=tz[P : 2 * P, :])
-        S.dma_start(out=l5[:], in_=offs5)
-        S.dma_start(out=wbw[:].bitcast(I32), in_=wb_words[0].bitcast(I32))
-
-        deal16(wp, ww)
-        deal16(w2p, w2w)
-        spread(wsc, wst)
-        deal8(nc.vector, wsp[:], wsc[:, 0:R])
-        spread(xs, xst)
-        nc.vector.tensor_copy(out=xsg[:], in_=xs[:].indirect(l1[:]))
-        nc.vector.tensor_copy(out=xg[:], in_=xw[:].indirect(l1[:]))
-        pa = [psum.tile([P, J], F32, name=f"pa{t}", tag=f"bank{t}") for t in range(4)]
-        for t in range(4):
-            nc.tensor.matmul_mx(out=pa[t][:], lhsT=wp[:, P * t : P * (t + 1)].bitcast(E2M1), lhsT_scale=wsp[:, P * t : P * (t + 1)],
-                                rhs=xg[:].bitcast(E5M2), rhs_scale=xsg[:], start=True, stop=True)
-        deal8(nc.vector, w2sp[:], wsc[:, R : 2 * R])
-        nc.vector.tensor_copy(out=osg[:], in_=os_[:].indirect(l2[:]))
-        nc.vector.tensor_copy(out=og[:], in_=ow[:].indirect(l2[:]))
-        pb = [psum.tile([P, J], F32, name=f"pb{t}", tag=f"bank{4 + t}") for t in range(4)]
-        for t in range(4):
-            nc.tensor.matmul_mx(out=pb[t][:], lhsT=w2p[:, P * t : P * (t + 1)].bitcast(E2M1), lhsT_scale=w2sp[:, P * t : P * (t + 1)],
-                                rhs=og[:].bitcast(E4M3), rhs_scale=osg[:], start=True, stop=True)
-        av[3] = reuse.tile([P, J], F32, name="av3", align_bytes=64, offset=4608)
-        av[2] = reuse.tile([P, J], F32, name="av2", align_bytes=64, offset=3584)
-        for t in range(4):
-            if t < 2:
-                nc.scalar.activation(out=av[t][:], in_=pa[t][:], func=COPY)
+        for t in range(PACK):
+            if t < A_ON_SCALAR:
+                nc.scalar.activation(out=a_rows[t][:], in_=a_banks[t][:], func=COPY)
             else:
-                nc.vector.tensor_copy(out=av[t][:], in_=pa[t][:])
-            nc.scalar.activation(out=ga[:, t, :], in_=av[t][:].indirect(l3[:]), func=COPY, scale=sat[:, t : t + 1])
-        for t in range(4):
-            nc.vector.tensor_copy(out=bv[t][:], in_=pb[t][:])
-            for lo, hi in ((0, O),) if t < 3 else ((0, O // 2), (O // 2, O)):
-                nc.scalar.activation(out=gb[:, t, lo:hi], in_=bv[t][:].indirect(l4[:, lo // 16 : hi // 16]), func=COPY, scale=sbt[:, t : t + 1])
-        gz = keep.tile([P, 2, O], F32, name="gz", tag="bv3", align_bytes=64)
-        for c in range(2):
-            nc.scalar.activation(out=gz[:, c, :], in_=tzt[c][:].indirect(l5[:]), func=COPY, scale=sot[:, c : c + 1])
-        for u, lo, hi in ((0, 0, O), (1, 0, O // 2), (1, O // 2, O)):
+                nc.vector.tensor_copy(out=a_rows[t][:], in_=a_banks[t][:])
+            nc.scalar.activation(
+                out=a_scaled[:, t, :], in_=a_rows[t][:].indirect(a_lists[:]), func=COPY, scale=sa_cols[:, t : t + 1]
+            )
+        for t in range(PACK):
+            nc.vector.tensor_copy(out=b_rows[t][:], in_=b_banks[t][:])
+            for lo, hi in HALVES if t == PACK - 1 else ((0, O),):
+                nc.scalar.activation(
+                    out=b_scaled[:, t, lo:hi], in_=b_rows[t][:].indirect(b_lists[:, lo // STRIPE : hi // STRIPE]),
+                    func=COPY, scale=sb_cols[:, t : t + 1],
+                )
+
+        floors = keep.tile([P, OUT_TILES, O], F32, name="floors", tag=f"b_rows{PACK - 1}", align_bytes=64)
+        for c in range(OUT_TILES):
+            nc.scalar.activation(
+                out=floors[:, c, :], in_=tz_rows[c][:].indirect(entry_list[:]), func=COPY, scale=so_cols[:, c : c + 1]
+            )
+
+        run = LINE // WORD
+        for t, (lo, hi) in ((0, (0, O)), (2, HALVES[0]), (2, HALVES[1])):
             nc.vector.tensor_tensor(
-                out=hb[:, lo:hi, 2 * u : 2 * u + 2].rearrange("p (c i) t -> p c t i", i=4),
-                in0=ga[:, 2 * u : 2 * u + 2, lo:hi].rearrange("p t (c i) -> p c t i", i=4),
-                in1=gb[:, 2 * u : 2 * u + 2, lo:hi].rearrange("p t (c i) -> p c t i", i=4),
+                out=hid[:, lo:hi, t : t + 2].rearrange("p (c i) t -> p c t i", i=run),
+                in0=a_scaled[:, t : t + 2, lo:hi].rearrange("p t (c i) -> p c t i", i=run),
+                in1=b_scaled[:, t : t + 2, lo:hi].rearrange("p t (c i) -> p c t i", i=run),
                 op=MAX,
             )
-        for lo, hi in ((0, O // 2), (O // 2, O)):
-            nc.vector.quantize_mx(out=hq[:, lo:hi].bitcast(E4M3), scales=hs[:, lo:hi], in_=hb[:, lo:hi, :].rearrange("p o t -> p (o t)"))
-        for c in range(2):
-            pp = psum.tile([P, O], F32, name=f"pp{c}", tag=f"bank{c}")
-            nc.tensor.matmul_mx(out=pp[:], lhsT=wbw[:, P * c : P * (c + 1)].bitcast(E2M1), lhsT_scale=wbs[:, P * c : P * (c + 1)],
-                                rhs=hq[:].bitcast(E4M3), rhs_scale=hs[:], start=True, stop=True)
-            nc.vector.tensor_tensor(out=res[c][:], in0=pp[:], in1=gz[:, c, :], op=MAX)
-            (S, A)[c].dma_start(out=out[P * c : P * (c + 1), :], in_=res[c][:])
+        for lo, hi in HALVES:
+            nc.vector.quantize_mx(
+                out=hid_words[:, lo:hi].bitcast(E4M3), scales=hid_plane[:, lo:hi],
+                in_=hid[:, lo:hi, :].rearrange("p o t -> p (o t)"),
+            )
+
+        for c, queue in enumerate((nc.sync, nc.scalar)):
+            cols = slice(P * c, P * (c + 1))
+            out_bank = psum.tile([P, O], F32, name=f"out_bank{c}", tag=f"bank{c}")
+            nc.tensor.matmul_mx(
+                out=out_bank[:], lhsT=wb_loaded[:, cols].bitcast(E2M1), lhsT_scale=wb_plane[:, cols],
+                rhs=hid_words[:].bitcast(E4M3), rhs_scale=hid_plane[:], start=True, stop=True,
+            )
+            nc.vector.tensor_tensor(out=result[c][:], in0=out_bank[:], in1=floors[:, c, :], op=MAX)
+            queue.dma_start(out=out[cols, :], in_=result[c][:])

from contextlib import ExitStack

import concourse.mybir as mybir

F32 = mybir.dt.float32
BF16 = mybir.dt.bfloat16
I32 = mybir.dt.int32
U32 = mybir.dt.uint32
U16 = mybir.dt.uint16
U8 = mybir.dt.uint8
E4M3 = mybir.dt.float8_e4m3fn_x4
E5M2 = mybir.dt.float8_e5m2_x4
E2M1 = mybir.dt.float4_e2m1fn_x4
COPY = mybir.ActivationFunctionType.Copy
MAX = mybir.AluOpType.max

P = 128
PACK = 4
QUADS = 4
QUAD = P // QUADS
ROWS = 4
STRIPE = 16
LINE = 16
WORD = 4
K = 512
T, J, R, O, N, E = 1024, 256, 512, 128, 256, 1024
HALVES = ((0, O // 2), (O // 2, O))
OUT_TILES = N // P
A_ON_SCALAR = 2
FLOPS = 2 * K * (2 * R * J + N * O)


def tile_list_groupmeet_twotab_one_stepfloor_kernel(
    tc, xt_words, xt_scales, w_words, w_scales, xo_words, xo_scales, w2_words, w2_scales,
    sa, sb, wb_words, wb_scales, tz, so, offs, offs2, offs3, offs4, offs5, out,
):
    nc = tc.nc
    with ExitStack() as ctx:
        keep = ctx.enter_context(tc.tile_pool(name="keep", bufs=1))
        psum = ctx.enter_context(tc.psum_pool(name="psum", bufs=1))

        def new(name, shape, dtype):
            return keep.tile(shape, dtype, name=name, align_bytes=64)

        token_list = new("token_list", [P, J // STRIPE], U16)
        note_list = new("note_list", [P, J // STRIPE], U16)
        a_lists = new("a_lists", [P, O // STRIPE], U16)
        b_lists = new("b_lists", [P, O // STRIPE], U16)
        entry_list = new("entry_list", [P, O // STRIPE], U16)
        xt_table = new("xt_table", [P, T], U32)
        reuse = ctx.enter_context(tc.tile_pool(name="reuse", bufs=1))
        xo_table_bytes = T * WORD
        xo_table = reuse.tile([P, T], U32, name="xo_table", align_bytes=64, offset=0)
        xo_plane = reuse.tile([P, T], U8, name="xo_plane", align_bytes=64, offset=xo_table_bytes)
        xt_plane = new("xt_plane", [P, T], U8)
        w_loaded = new("w_loaded", [P, R], U16)
        w2_loaded = new("w2_loaded", [P, R], U16)
        wb_loaded = new("wb_loaded", [P, N], U16)
        wb_plane = new("wb_plane", [P, N], U8)
        sa_cols = new("sa_cols", [P, PACK], F32)
        sb_cols = new("sb_cols", [P, PACK], F32)
        so_cols = new("so_cols", [P, OUT_TILES], F32)
        tz_rows = [new(f"tz_rows{c}", [P, E], F32) for c in range(OUT_TILES)]
        w_dealt = new("w_dealt", [P, R], U16)
        w2_dealt = new("w2_dealt", [P, R], U16)
        w_plane_dealt = new("w_plane_dealt", [P, R], U8)
        w2_plane_dealt = new("w2_plane_dealt", [P, R], U8)
        xt_picked = new("xt_picked", [P, J], U32)
        xo_picked = new("xo_picked", [P, J], U32)
        xt_plane_picked = new("xt_plane_picked", [P, J], U8)
        xo_plane_picked = new("xo_plane_picked", [P, J], U8)
        a_scaled = new("a_scaled", [P, PACK, O], F32)
        b_scaled = new("b_scaled", [P, PACK, O], F32)
        hid = new("hid", [P, O, PACK], BF16)
        hid_words = new("hid_words", [P, O], U32)
        hid_plane = new("hid_plane", [P, O], U8)
        a_rows = [new(f"a_rows{t}", [P, J], F32) for t in range(A_ON_SCALAR)]
        b_rows = [new(f"b_rows{t}", [P, J], F32) for t in range(PACK)]
        result = [new(f"result{c}", [P, O], F32) for c in range(OUT_TILES)]
        w_planes = new("w_planes", [P, 2 * R], U8)
        w_stage = new("w_stage", [ROWS, QUADS, 2 * R // WORD], I32)
        xt_stage = new("xt_stage", [P // 2 + ROWS, 2, T // WORD], I32)

        for plane in (xt_plane, w_planes, xo_plane, wb_plane):
            nc.vector.memset(plane[:].bitcast(I32), 0)

        def load_fp8_words(dst, src):
            nc.sync.dma_start(out=dst[:].bitcast(I32), in_=src[0].rearrange("p n t -> p (n t)").bitcast(I32))

        def load_fp4_words(dst, src):
            nc.sync.dma_start(out=dst[:].bitcast(I32), in_=src[0].bitcast(I32))

        def load_plane(dst, src):
            for q in range(QUADS):
                nc.sync.dma_start(
                    out=dst[QUAD * q : QUAD * q + ROWS, :].bitcast(I32),
                    in_=src[0, ROWS * q : ROWS * (q + 1), :].bitcast(I32),
                )

        def stage(queue, dst, rows):
            queue.dma_start(out=dst, in_=rows.bitcast(I32).rearrange("(q r) n -> r q n", r=ROWS))

        def deal(copy, dst, src, run):
            copy(
                out=dst.rearrange("p (t c i) -> p c t i", t=PACK, i=run),
                in_=src.rearrange("p (c i t) -> p c t i", t=PACK, i=run),
            )

        def products(banks, words, plane, picked, picked_plane):
            for t in range(PACK):
                cols = slice(P * t, P * (t + 1))
                nc.tensor.matmul_mx(
                    out=banks[t][:], lhsT=words[:, cols].bitcast(E2M1), lhsT_scale=plane[:, cols],
                    rhs=picked, rhs_scale=picked_plane[:], start=True, stop=True,
                )

        for h, queue in enumerate((nc.sync, nc.scalar)):
            stage(queue, xt_stage[P // 2 * h : P // 2 * h + ROWS], xt_scales[0, 2 * ROWS * h : 2 * ROWS * (h + 1)])
        stage(nc.sync, w_stage[:, :, 0 : R // WORD], w_scales[0])
        stage(nc.scalar, w_stage[:, :, R // WORD :], w2_scales[0])
        nc.sync.dma_start(out=token_list[:], in_=offs)
        load_fp4_words(w_loaded, w_words)
        load_fp8_words(xt_table, xt_words)
        load_fp4_words(w2_loaded, w2_words)
        nc.gpsimd.dma_start(out=sa_cols[:], in_=sa.rearrange("(p t) o -> p (t o)", t=PACK))
        nc.gpsimd.dma_start(out=sb_cols[:], in_=sb.rearrange("(p t) o -> p (t o)", t=PACK))
        with nc.allow_non_contiguous_dma(reason="one step for each partition and output tile"):
            nc.gpsimd.dma_start(out=so_cols[:], in_=so.rearrange("(c p) o -> p (c o)", c=OUT_TILES))
        load_fp8_words(xo_table, xo_words)
        nc.sync.dma_start(out=note_list[:], in_=offs2)
        load_plane(xo_plane, xo_scales)
        nc.sync.dma_start(out=a_lists[:], in_=offs3)
        nc.sync.dma_start(out=b_lists[:], in_=offs4)
        nc.sync.dma_start(out=tz_rows[0][:], in_=tz[0:P, :])
        load_plane(wb_plane, wb_scales)
        nc.sync.dma_start(out=tz_rows[1][:], in_=tz[P : 2 * P, :])
        nc.sync.dma_start(out=entry_list[:], in_=offs5)
        load_fp4_words(wb_loaded, wb_words)

        deal(nc.scalar.copy, w_dealt[:], w_loaded[:], LINE // 2)
        deal(nc.scalar.copy, w2_dealt[:], w2_loaded[:], LINE // 2)
        for q in range(QUADS):
            h, s = divmod(q, 2)
            nc.vector.tensor_copy(
                out=xt_plane[QUAD * q : QUAD * q + ROWS, :].bitcast(I32),
                in_=xt_stage[P // 2 * h : P // 2 * h + ROWS, s],
            )
        for q in range(QUADS):
            nc.vector.tensor_copy(out=w_planes[QUAD * q : QUAD * q + ROWS, :].bitcast(I32), in_=w_stage[:, q])
        nc.vector.tensor_copy(out=xt_plane_picked[:], in_=xt_plane[:].indirect(token_list[:]))
        deal(nc.vector.tensor_copy, w_plane_dealt[:], w_planes[:, 0:R], LINE)
        nc.vector.tensor_copy(out=xt_picked[:], in_=xt_table[:].indirect(token_list[:]))
        a_banks = [psum.tile([P, J], F32, name=f"a_bank{t}", tag=f"bank{t}") for t in range(PACK)]
        products(a_banks, w_dealt, w_plane_dealt, xt_picked[:].bitcast(E5M2), xt_plane_picked)

        deal(nc.vector.tensor_copy, w2_plane_dealt[:], w_planes[:, R : 2 * R], LINE)
        nc.vector.tensor_copy(out=xo_plane_picked[:], in_=xo_plane[:].indirect(note_list[:]))
        nc.vector.tensor_copy(out=xo_picked[:], in_=xo_table[:].indirect(note_list[:]))
        b_banks = [psum.tile([P, J], F32, name=f"b_bank{t}", tag=f"bank{PACK + t}") for t in range(PACK)]
        products(b_banks, w2_dealt, w2_plane_dealt, xo_picked[:].bitcast(E4M3), xo_plane_picked)

        first_offset = xo_table_bytes - T // 2
        last_a = reuse.tile([P, J], F32, name="a_rows3", align_bytes=64, offset=first_offset + J * WORD)
        third_a = reuse.tile([P, J], F32, name="a_rows2", align_bytes=64, offset=first_offset)
        a_rows.extend([third_a, last_a])

        for t in range(PACK):
            if t < A_ON_SCALAR:
                nc.scalar.activation(out=a_rows[t][:], in_=a_banks[t][:], func=COPY)
            else:
                nc.vector.tensor_copy(out=a_rows[t][:], in_=a_banks[t][:])
            nc.scalar.activation(
                out=a_scaled[:, t, :], in_=a_rows[t][:].indirect(a_lists[:]), func=COPY, scale=sa_cols[:, t : t + 1]
            )
        for t in range(PACK):
            nc.vector.tensor_copy(out=b_rows[t][:], in_=b_banks[t][:])
            for lo, hi in HALVES if t == PACK - 1 else ((0, O),):
                nc.scalar.activation(
                    out=b_scaled[:, t, lo:hi], in_=b_rows[t][:].indirect(b_lists[:, lo // STRIPE : hi // STRIPE]),
                    func=COPY, scale=sb_cols[:, t : t + 1],
                )

        floors = keep.tile([P, OUT_TILES, O], F32, name="floors", tag=f"b_rows{PACK - 1}", align_bytes=64)
        for c in range(OUT_TILES):
            nc.scalar.activation(
                out=floors[:, c, :], in_=tz_rows[c][:].indirect(entry_list[:]), func=COPY, scale=so_cols[:, c : c + 1]
            )

        run = LINE // WORD
        for t, (lo, hi) in ((0, (0, O)), (2, HALVES[0]), (2, HALVES[1])):
            nc.vector.tensor_tensor(
                out=hid[:, lo:hi, t : t + 2].rearrange("p (c i) t -> p c t i", i=run),
                in0=a_scaled[:, t : t + 2, lo:hi].rearrange("p t (c i) -> p c t i", i=run),
                in1=b_scaled[:, t : t + 2, lo:hi].rearrange("p t (c i) -> p c t i", i=run),
                op=MAX,
            )
        for lo, hi in HALVES:
            nc.vector.quantize_mx(
                out=hid_words[:, lo:hi].bitcast(E4M3), scales=hid_plane[:, lo:hi],
                in_=hid[:, lo:hi, :].rearrange("p o t -> p (o t)"),
            )

        for c, queue in enumerate((nc.sync, nc.scalar)):
            cols = slice(P * c, P * (c + 1))
            out_bank = psum.tile([P, O], F32, name=f"out_bank{c}", tag=f"bank{c}")
            nc.tensor.matmul_mx(
                out=out_bank[:], lhsT=wb_loaded[:, cols].bitcast(E2M1), lhsT_scale=wb_plane[:, cols],
                rhs=hid_words[:].bitcast(E4M3), rhs_scale=hid_plane[:], start=True, stop=True,
            )
            nc.vector.tensor_tensor(out=result[c][:], in0=out_bank[:], in1=floors[:, c, :], op=MAX)
            queue.dma_start(out=out[cols, :], in_=result[c][:])
